import numpy as np, ml_dtypes
CORES = [24,48,72,152,176,200]
N = 6
import mx_ref
NC, KB = 128, 1
BF = ml_dtypes.bfloat16
def cut(t, i, w=512):
    return t[:, w * i:w * i + w]
def term(a, B):
    return np.stack([mx_ref.matmul(mx_ref.quantize(cut(a, i)), B) for i in range(4)], axis=2).reshape(128, -1)
def setup_inputs(rng):
    def f(*shape):
        return mx_ref.flush((rng.standard_normal(shape, dtype=np.float32) * np.exp2(rng.integers(-2, 3, shape[:-1] + (1,)))).astype(BF))
    return {"a": f(N, 128, 4 * 512), "b": f(N, 128, KB * 4 * NC)}
def setup_inputs_blocks(rng):
    d = setup_inputs(rng)
    for k in ("a", "b"): d[k] = mx_ref.spread(d[k], rng, 2)
    return d
def setup_inputs_wide(rng):
    d = setup_inputs(rng)
    for k in ("a", "b"): d[k] = mx_ref.flush((d[k].astype(np.float32) * np.exp2(rng.integers(-4, 5, (N, 1, 1))).astype(np.float32)).astype(BF))
    return d
def setup_inputs_lossless(rng):
    a = np.zeros((N, 128, 4 * 128, 4), np.float32)
    for r in range(N):
        k = rng.integers(0, 512, size=4 * 128)
        a[r, k // 4, np.arange(4 * 128), k % 4] = 1.0
    size = np.repeat(2.0 ** rng.integers(-4, 5, size=(1, 1, (KB * 4 * NC) // 4)), 4, axis=2)
    b = rng.integers(-1, 2, size=(N, 128, KB * 4 * NC)) * size
    return {"a": a.reshape(N, 128, 4 * 512).astype(BF), "b": b.astype(np.float32).astype(BF)}
def reference(a, b):
    y = np.zeros((N, 128, KB * 4 * NC), np.float32)
    for k in range(KB):
        y[:, :, 4 * NC * k:4 * NC * k + 4 * NC] = mx_ref.total([term(a[r], mx_ref.quantize(cut(b[r], k, 4 * NC))) for r in range(N)])
    return {"y": y}

@@ -1,0 +1,247 @@
+from concourse.bass import DstId, RemoteDMATransfer
+from concourse.mybir import dt, AluOpType, ActivationFunctionType
+
+WORLD = 256
+NC = 128
+HALF = NC // 2
+W = 4 * NC
+BANK = 512
+
+_CODES, _PLANE = "float8_e4m3fn_x4", "uint8"
+SCRATCH = {
+    "a_sb": ("sbuf", [128, 4 * W], "bfloat16"), "b_sb": ("sbuf", [128, W], "bfloat16"),
+    "aq": ("sbuf", [128, 4 * NC], _CODES), "asc": ("sbuf", [128, 4 * NC], _PLANE),
+    "bq": ("sbuf", [128, NC], _CODES), "bsc": ("sbuf", [128, NC], _PLANE),
+    "diag": ("sbuf", [128, W + 4], "bfloat16"),
+    "selq": ("sbuf", [128, 4 * NC], _CODES), "selsc": ("sbuf", [128, 4 * NC], _PLANE),
+    "t_bf": ("sbuf", [128, W], "bfloat16"), "tq": ("sbuf", [128, NC], _CODES), "tsc": ("sbuf", [128, NC], _PLANE),
+    "o_bf": ("sbuf", [128, W], "bfloat16"), "oq": ("sbuf", [128, NC], _CODES), "osc": ("sbuf", [128, NC], _PLANE),
+    "r1q": ("sbuf", [128, NC], _CODES), "r1sc": ("sbuf", [128, NC], _PLANE),
+    "r2q": ("sbuf", [128, NC], _CODES), "r2sc": ("sbuf", [128, NC], _PLANE),
+    "r3q": ("sbuf", [128, NC], _CODES), "r3sc": ("sbuf", [128, NC], _PLANE),
+    "eq": ("sbuf", [128, NC], _CODES), "esc": ("sbuf", [128, NC], _PLANE),
+    "fq": ("sbuf", [128, NC], _CODES), "fsc": ("sbuf", [128, NC], _PLANE),
+    "y_sb": ("sbuf", [128, W], "float32"),
+    "ps": ("psum", [128, 8 * BANK], "float32"),
+}
+SEMAPHORES = (["ones", "sel", "selq", "ld_b", "bq", "tq", "oq", "cp1a", "cp1v", "cp2a", "cp2v", "cp3a", "cp3v",
+               "r1", "r2", "r3", "e", "fp", "fc", "f", "ydone", "sent"]
+              + ["ld_a%d" % i for i in range(4)] + ["aq%d" % i for i in range(4)]
+              + ["g1_%d" % i for i in range(4)] + ["g2_%d" % i for i in range(4)] + ["g3_%d" % i for i in range(4)])
+
+
+def _bits(mask):
+    return [e for e in range(16) if (mask >> e) & 1]
+
+
+def _mask(engines):
+    m = 0
+    for e in engines:
+        m |= 1 << e
+    return m
+
+
+def _plan(T, topo):
+    cores = list(T.cores)
+    hosts = sorted({topo.host(c) for c in cores})
+    pair, single, relay, adder = {}, {}, {}, {}
+    for h in hosts:
+        mine = [c for c in cores if topo.host(c) == h]
+        pair[h] = [[x, y] for x in mine for y in mine if x < y and topo.may_write(x, y) and topo.may_write(y, x)][0]
+        single[h] = [c for c in mine if c not in pair[h]][0]
+
+        def beside(c):
+            return [k for k in range(WORLD) if k != c and topo.host(k) == h and topo.chip(k) == topo.chip(c)]
+        relay[h] = [[k for k in beside(x) if topo.die(k) == topo.die(x) and topo.may_write(k, single[h])][0]
+                    for x in pair[h]]
+        s = single[h]
+        adder[h] = [k for k in beside(s) if topo.die(k) != topo.die(s)
+                    and all(topo.may_write(k, x) for x in pair[h])][0]
+    return hosts, pair, single, relay, adder
+
+
+def rank_program(g, core, T, topo):
+    hosts, pair, single, relay, adder = _plan(T, topo)
+    h = topo.host(core)
+    if h not in hosts:
+        return
+    o = [x for x in hosts if x != h][0]
+    S = T.sem
+    sent = [0]
+
+    def codes(buf, lo=0, hi=NC):
+        return buf[:, lo:hi].bitcast(dt.uint8)
+
+    def send(dests, src, dst):
+        if len(dests) == 1:
+            d, engines, sem = dests[0]
+            rid, pid = topo.addr(d, core)
+            g.remote_dma(out_ap=dst, in_ap=src, remote_sem=sem, local_sem=S.sent, pid=pid, routing_id=rid,
+                         dma_engine_mask=_mask(engines))
+            sent[0] += len(engines)
+            return
+        tr = []
+        for d, engines, sem in dests:
+            rid, pid = topo.addr(d, core)
+            tr.append(RemoteDMATransfer(dst_ids=[DstId(rid=rid, pnc=pid)], dma_engine_mask=_mask(engines),
+                                        remote_sem=sem, src=src, dst=dst))
+            sent[0] += len(engines)
+        g.remote_dma_fused(tr, local_sem=S.sent)
+
+    def tile(dests, sq, ssc, dq, dsc, lo=0, hi=NC):
+        send(dests, ssc[:, lo:hi], dsc[:, lo:hi])
+        send(dests, codes(sq, lo, hi), codes(dq, lo, hi))
+
+    def far_near(far, near):
+        f = _bits(topo.mask(core, far))
+        return f, [e for e in _bits(topo.mask(core, near)) if e not in f]
+
+    def bank(k):
+        return T.ps[:, BANK * k:BANK * k + NC]
+
+    def selectors():
+        g.vector.memset(T.diag[:], 1.0).then_inc(S.ones, 1)
+        g.wait_ge(S.ones, 1)
+        g.affine_select(T.diag[:], T.diag[:], [[-1, W + 4]], AluOpType.is_equal, 0.0, 3, 4).then_inc(S.sel, 1)
+        g.vector.wait_ge(S.sel, 1)
+        for i in range(4):
+            g.vector.quantize_mx(T.selq[:, NC * i:NC * i + NC], T.selsc[:, NC * i:NC * i + NC],
+                                 T.diag[:, 3 - i:3 - i + W]).then_inc(S.selq, 1)
+
+    def unpack(i, k, q, sc, start, stop):
+        return g.tensor.matmul_mx(bank(k), T.selq[:, NC * i:NC * i + NC], T.selsc[:, NC * i:NC * i + NC],
+                                  q[:], sc[:], start, stop)
+
+    def product(i, k, stop):
+        return g.tensor.matmul_mx(bank(k), T.aq[:, NC * i:NC * i + NC], T.asc[:, NC * i:NC * i + NC],
+                                  T.bq[:], T.bsc[:], True, stop)
+
+    def gather(out, base, done, sa, sv):
+        for i in (0, 2):
+            g.scalar.wait_ge(S[done % i], 1)
+            g.scalar.activation(out[:, i:W:4], bank(base + i), ActivationFunctionType.Copy).then_inc(sa, 1)
+        for i in (1, 3):
+            g.vector.wait_ge(S[done % i], 1)
+            g.vector.tensor_copy(out[:, i:W:4], bank(base + i)).then_inc(sv, 1)
+
+    if core in relay[h]:
+        k = relay[h].index(core)
+        own, peer, s = pair[h][k], pair[h][1 - k], single[h]
+        far, near = far_near(s, own)
+        lo, hi = HALF * k, HALF * k + HALF
+        g.wait_ge(S.r1, 2 * len(near))
+        tile([(s, far, (S.r2, S.r3)[k])], T.r1q, T.r1sc, (T.r2q, T.r3q)[k], (T.r2sc, T.r3sc)[k])
+        two = [(s, far[:len(far) // 2], S.f), (peer, far[len(far) // 2:], S.f)]
+        g.wait_ge(S.fp, len(far))
+        send(two, T.fsc[:, lo:hi], T.fsc[:, lo:hi])
+        g.wait_ge(S.fc, len(far))
+        send(two, codes(T.fq, lo, hi), codes(T.fq, lo, hi))
+        tile([(own, near, S.f)], T.fq, T.fsc, T.fq, T.fsc, lo, hi)
+        g.wait_ge(S.sent, sent[0])
+        return
+
+    if core == adder[h]:
+        s = single[h]
+        far, near = far_near(pair[h][0], s)
+        selectors()
+        g.tensor.wait_ge(S.selq, 4)
+        g.tensor.wait_ge(S.r1, 2 * len(near))
+        for i in range(4):
+            unpack(i, i, T.r1q, T.r1sc, True, False)
+        g.tensor.wait_ge(S.r2, 2 * len(far))
+        for i in range(4):
+            unpack(i, i, T.r2q, T.r2sc, False, True).then_inc(S["g1_%d" % i], 1)
+        gather(T.o_bf, 0, "g1_%d", S.cp2a, S.cp2v)
+        g.vector.wait_ge(S.cp2a, 2)
+        g.vector.wait_ge(S.cp2v, 2)
+        g.vector.quantize_mx(T.oq[:], T.osc[:], T.o_bf[:]).then_inc(S.oq, 1)
+        g.wait_ge(S.r2, 2 * len(far))
+        tile([(s, near, S.r1)], T.r2q, T.r2sc, T.r1q, T.r1sc)
+        g.wait_ge(S.oq, 1)
+        tile([(pair[h][0], far[:len(far) // 2], S.e), (pair[h][1], far[len(far) // 2:], S.e)],
+             T.oq, T.osc, T.eq, T.esc)
+        g.wait_ge(S.sent, sent[0])
+        return
+
+    if T.rank_of(core) is None:
+        return
+
+    def piece(t, i):
+        return t[:, W * i:W * i + W]
+    g.sync.dma_start(T.b_sb[:], T.b[:]).then_inc(S.ld_b, 16)
+    g.scalar.dma_start(piece(T.a_sb, 0), piece(T.a, 0)).then_inc(S.ld_a0, 16)
+    g.sync.dma_start(piece(T.a_sb, 1), piece(T.a, 1)).then_inc(S.ld_a1, 16)
+    g.scalar.dma_start(piece(T.a_sb, 2), piece(T.a, 2)).then_inc(S.ld_a2, 16)
+    g.sync.dma_start(piece(T.a_sb, 3), piece(T.a, 3)).then_inc(S.ld_a3, 16)
+    selectors()
+    g.vector.wait_ge(S.ld_b, 16)
+    g.vector.quantize_mx(T.bq[:], T.bsc[:], T.b_sb[:]).then_inc(S.bq, 1)
+    g.tensor.wait_ge(S.bq, 1)
+    for i in range(4):
+        g.vector.wait_ge(S["ld_a%d" % i], 16)
+        g.vector.quantize_mx(T.aq[:, NC * i:NC * i + NC], T.asc[:, NC * i:NC * i + NC],
+                             piece(T.a_sb, i)).then_inc(S["aq%d" % i], 1)
+        g.tensor.wait_ge(S["aq%d" % i], 1)
+        product(i, i, True).then_inc(S["g1_%d" % i], 1)
+    for i in range(3):
+        g.scalar.wait_ge(S["g1_%d" % i], 1)
+        g.scalar.activation(T.t_bf[:, i:W:4], bank(i), ActivationFunctionType.Copy).then_inc(S.cp1a, 1)
+    g.vector.wait_ge(S.g1_3, 1)
+    g.vector.tensor_copy(T.t_bf[:, 3:W:4], bank(3)).then_inc(S.cp1v, 1)
+    g.vector.wait_ge(S.cp1v, 1)
+    g.vector.wait_ge(S.cp1a, 3)
+    g.vector.quantize_mx(T.tq[:], T.tsc[:], T.t_bf[:]).then_inc(S.tq, 1)
+    for i in range(4):
+        product(i, 4 + i, False)
+    g.tensor.wait_ge(S.selq, 4)
+    g.wait_ge(S.tq, 1)
+
+    if core in pair[h]:
+        k = pair[h].index(core)
+        peer = pair[h][1 - k]
+        far, near = far_near(peer, relay[h][k])
+        lo, hi = HALF * k, HALF * k + HALF
+        tile([(peer, far, S.r1)], T.tq, T.tsc, T.r1q, T.r1sc)
+        tile([(relay[h][k], near, S.r1)], T.tq, T.tsc, T.r1q, T.r1sc)
+        g.tensor.wait_ge(S.r1, 2 * len(far))
+        for i in range(4):
+            unpack(i, 4 + i, T.r1q, T.r1sc, False, True).then_inc(S["g2_%d" % i], 1)
+        gather(T.o_bf, 4, "g2_%d", S.cp2a, S.cp2v)
+        g.vector.wait_ge(S.cp2a, 2)
+        g.vector.wait_ge(S.cp2v, 2)
+        g.vector.quantize_mx(T.oq[:], T.osc[:], T.o_bf[:]).then_inc(S.oq, 1)
+        g.wait_ge(S.oq, 1)
+        send([(relay[o][k], far, S.fp)], T.osc[:, lo:hi], T.fsc[:, lo:hi])
+        send([(relay[o][k], far, S.fc)], codes(T.oq, lo, hi), codes(T.fq, lo, hi))
+        g.tensor.wait_ge(S.cp1a, 3)
+        g.tensor.wait_ge(S.cp1v, 1)
+        for i in range(4):
+            product(i, i, False)
+            unpack(i, i, T.r1q, T.r1sc, False, False)
+        g.tensor.wait_ge(S.e, len(far))
+        for i in range(4):
+            unpack(i, i, T.eq, T.esc, False, False)
+        g.tensor.wait_ge(S.f, 2 * len(near) + len(far))
+        for i in range(4):
+            unpack(i, i, T.fq, T.fsc, False, True).then_inc(S["g3_%d" % i], 1)
+        base = 0
+    else:
+        far, near = far_near(adder[o], adder[h])
+        tile([(adder[o], far, S.r2)], T.tq, T.tsc, T.r2q, T.r2sc)
+        tile([(adder[h], near, S.r1)], T.tq, T.tsc, T.r1q, T.r1sc)
+        for sem, n, q, sc in ((S.r1, 2 * len(near), T.r1q, T.r1sc), (S.r2, 2 * len(far), T.r2q, T.r2sc),
+                              (S.r3, 2 * len(far), T.r3q, T.r3sc)):
+            g.tensor.wait_ge(sem, n)
+            for i in range(4):
+                unpack(i, 4 + i, q, sc, False, False)
+        g.tensor.wait_ge(S.f, 2 * len(far))
+        for i in range(4):
+            unpack(i, 4 + i, T.fq, T.fsc, False, True).then_inc(S["g3_%d" % i], 1)
+        base = 4
+
+    gather(T.y_sb, base, "g3_%d", S.cp3a, S.cp3v)
+    g.sync.wait_ge(S.cp3a, 2)
+    g.sync.wait_ge(S.cp3v, 2)
+    g.sync.dma_start(T.y[:], T.y_sb[:]).then_inc(S.ydone, 16)
+    g.sync.wait_ge(S.ydone, 16)
+    g.wait_ge(S.sent, sent[0])

@@ -14,18 +14,21 @@ SCRATCH = {
     "bq": ("sbuf", [128, NC], _CODES), "bsc": ("sbuf", [128, NC], _PLANE),
     "diag": ("sbuf", [128, W + 4], "bfloat16"),
     "selq": ("sbuf", [128, 4 * NC], _CODES), "selsc": ("sbuf", [128, 4 * NC], _PLANE),
+    "te_bf": ("sbuf", [128, W], "bfloat16"), "teq": ("sbuf", [128, NC], _CODES), "tesc": ("sbuf", [128, NC], _PLANE),
     "t_bf": ("sbuf", [128, W], "bfloat16"), "tq": ("sbuf", [128, NC], _CODES), "tsc": ("sbuf", [128, NC], _PLANE),
     "o_bf": ("sbuf", [128, W], "bfloat16"), "oq": ("sbuf", [128, NC], _CODES), "osc": ("sbuf", [128, NC], _PLANE),
     "r1q": ("sbuf", [128, NC], _CODES), "r1sc": ("sbuf", [128, NC], _PLANE),
     "r2q": ("sbuf", [128, NC], _CODES), "r2sc": ("sbuf", [128, NC], _PLANE),
     "r3q": ("sbuf", [128, NC], _CODES), "r3sc": ("sbuf", [128, NC], _PLANE),
+    "nq": ("sbuf", [128, NC], _CODES), "nsc": ("sbuf", [128, NC], _PLANE),
     "eq": ("sbuf", [128, NC], _CODES), "esc": ("sbuf", [128, NC], _PLANE),
+    "e2q": ("sbuf", [128, NC], _CODES), "e2sc": ("sbuf", [128, NC], _PLANE),
     "fq": ("sbuf", [128, NC], _CODES), "fsc": ("sbuf", [128, NC], _PLANE),
     "y_sb": ("sbuf", [128, W], "float32"),
     "ps": ("psum", [128, 8 * BANK], "float32"),
 }
-SEMAPHORES = (["ones", "sel", "selq", "ld_b", "bq", "tq", "oq", "cp1a", "cp1v", "cp2a", "cp2v", "cp3a", "cp3v",
-               "r1", "r2", "r3", "e", "fp", "fc", "f", "ydone", "sent"]
+SEMAPHORES = (["ones", "sel", "selq", "selq2", "z1", "z2", "ld_b", "bq", "teq", "tq", "oq", "cpe", "cp1a", "cp1v",
+               "cp2a", "cp2v", "cp3a", "cp3v", "r1", "r2", "r3", "n", "e", "e2", "fp", "f", "ydone", "sent"]
               + ["ld_a%d" % i for i in range(4)] + ["aq%d" % i for i in range(4)]
               + ["g1_%d" % i for i in range(4)] + ["g2_%d" % i for i in range(4)] + ["g3_%d" % i for i in range(4)])
 
@@ -44,7 +47,7 @@ def _mask(engines):
 def _plan(T, topo):
     cores = list(T.cores)
     hosts = sorted({topo.host(c) for c in cores})
-    pair, single, relay, adder = {}, {}, {}, {}
+    pair, single, relay, passer = {}, {}, {}, {}
     for h in hosts:
         mine = [c for c in cores if topo.host(c) == h]
         pair[h] = [[x, y] for x in mine for y in mine if x < y and topo.may_write(x, y) and topo.may_write(y, x)][0]
@@ -52,22 +55,23 @@ def _plan(T, topo):
 
         def beside(c):
             return [k for k in range(WORLD) if k != c and topo.host(k) == h and topo.chip(k) == topo.chip(c)]
-        relay[h] = [[k for k in beside(x) if topo.die(k) == topo.die(x) and topo.may_write(k, single[h])][0]
+        relay[h] = [[k for k in beside(x) if topo.die(k) == topo.die(x) and topo.may_write(k, single[h])][:2]
                     for x in pair[h]]
         s = single[h]
-        adder[h] = [k for k in beside(s) if topo.die(k) != topo.die(s)
-                    and all(topo.may_write(k, x) for x in pair[h])][0]
-    return hosts, pair, single, relay, adder
+        ok = [k for k in beside(s) if all(topo.may_write(k, x) for x in pair[h])]
+        passer[h] = ([k for k in ok if topo.die(k) != topo.die(s)][:2], [k for k in ok if topo.die(k) == topo.die(s)][:2])
+    return hosts, pair, single, relay, passer
 
 
 def rank_program(g, core, T, topo):
-    hosts, pair, single, relay, adder = _plan(T, topo)
+    hosts, pair, single, relay, passer = _plan(T, topo)
     h = topo.host(core)
     if h not in hosts:
         return
     o = [x for x in hosts if x != h][0]
     S = T.sem
     sent = [0]
+    COPY = ActivationFunctionType.Copy
 
     def codes(buf, lo=0, hi=NC):
         return buf[:, lo:hi].bitcast(dt.uint8)
@@ -96,17 +100,17 @@ def rank_program(g, core, T, topo):
         f = _bits(topo.mask(core, far))
         return f, [e for e in _bits(topo.mask(core, near)) if e not in f]
 
-    def bank(k):
-        return T.ps[:, BANK * k:BANK * k + NC]
+    def bank(k, lo=0, hi=NC):
+        return T.ps[:, BANK * k + lo:BANK * k + hi]
 
-    def selectors():
+    def diagonal():
         g.vector.memset(T.diag[:], 1.0).then_inc(S.ones, 1)
         g.wait_ge(S.ones, 1)
         g.affine_select(T.diag[:], T.diag[:], [[-1, W + 4]], AluOpType.is_equal, 0.0, 3, 4).then_inc(S.sel, 1)
-        g.vector.wait_ge(S.sel, 1)
-        for i in range(4):
-            g.vector.quantize_mx(T.selq[:, NC * i:NC * i + NC], T.selsc[:, NC * i:NC * i + NC],
-                                 T.diag[:, 3 - i:3 - i + W]).then_inc(S.selq, 1)
+
+    def selector(i, sem):
+        g.vector.quantize_mx(T.selq[:, NC * i:NC * i + NC], T.selsc[:, NC * i:NC * i + NC],
+                             T.diag[:, 3 - i:3 - i + W]).then_inc(sem, 1)
 
     def unpack(i, k, q, sc, start, stop):
         return g.tensor.matmul_mx(bank(k), T.selq[:, NC * i:NC * i + NC], T.selsc[:, NC * i:NC * i + NC],
@@ -116,119 +120,163 @@ def rank_program(g, core, T, topo):
         return g.tensor.matmul_mx(bank(k), T.aq[:, NC * i:NC * i + NC], T.asc[:, NC * i:NC * i + NC],
                                   T.bq[:], T.bsc[:], True, stop)
 
-    def gather(out, base, done, sa, sv):
-        for i in (0, 2):
-            g.scalar.wait_ge(S[done % i], 1)
-            g.scalar.activation(out[:, i:W:4], bank(base + i), ActivationFunctionType.Copy).then_inc(sa, 1)
-        for i in (1, 3):
-            g.vector.wait_ge(S[done % i], 1)
-            g.vector.tensor_copy(out[:, i:W:4], bank(base + i)).then_inc(sv, 1)
+    def place(t, i):
+        return t[:, (W // 2) * (i // 2) + i % 2:(W // 2) * (i // 2) + W // 2:2]
 
-    if core in relay[h]:
-        k = relay[h].index(core)
-        own, peer, s = pair[h][k], pair[h][1 - k], single[h]
-        far, near = far_near(s, own)
-        lo, hi = HALF * k, HALF * k + HALF
-        g.wait_ge(S.r1, 2 * len(near))
-        tile([(s, far, (S.r2, S.r3)[k])], T.r1q, T.r1sc, (T.r2q, T.r3q)[k], (T.r2sc, T.r3sc)[k])
-        two = [(s, far[:len(far) // 2], S.f), (peer, far[len(far) // 2:], S.f)]
-        g.wait_ge(S.fp, len(far))
-        send(two, T.fsc[:, lo:hi], T.fsc[:, lo:hi])
-        g.wait_ge(S.fc, len(far))
-        send(two, codes(T.fq, lo, hi), codes(T.fq, lo, hi))
-        tile([(own, near, S.f)], T.fq, T.fsc, T.fq, T.fsc, lo, hi)
-        g.wait_ge(S.sent, sent[0])
-        return
+    for k in range(2):
+        if core in relay[h][k]:
+            j = relay[h][k].index(core)
+            own, peer, s = pair[h][k], pair[h][1 - k], single[h]
+            far, near = far_near(s, own)
+            lo, hi = HALF * k, HALF * k + HALF
 
-    if core == adder[h]:
-        s = single[h]
-        far, near = far_near(pair[h][0], s)
-        selectors()
-        g.tensor.wait_ge(S.selq, 4)
-        g.tensor.wait_ge(S.r1, 2 * len(near))
-        for i in range(4):
-            unpack(i, i, T.r1q, T.r1sc, True, False)
-        g.tensor.wait_ge(S.r2, 2 * len(far))
-        for i in range(4):
-            unpack(i, i, T.r2q, T.r2sc, False, True).then_inc(S["g1_%d" % i], 1)
-        gather(T.o_bf, 0, "g1_%d", S.cp2a, S.cp2v)
-        g.vector.wait_ge(S.cp2a, 2)
-        g.vector.wait_ge(S.cp2v, 2)
-        g.vector.quantize_mx(T.oq[:], T.osc[:], T.o_bf[:]).then_inc(S.oq, 1)
-        g.wait_ge(S.r2, 2 * len(far))
-        tile([(s, near, S.r1)], T.r2q, T.r2sc, T.r1q, T.r1sc)
-        g.wait_ge(S.oq, 1)
-        tile([(pair[h][0], far[:len(far) // 2], S.e), (pair[h][1], far[len(far) // 2:], S.e)],
-             T.oq, T.osc, T.eq, T.esc)
-        g.wait_ge(S.sent, sent[0])
-        return
+            def part(q, sc, a=0, b=NC):
+                return sc[:, a:b] if j == 0 else codes(q, a, b)
+            g.wait_ge(S.r1, len(near))
+            send([(s, far, (S.r2, S.r3)[k])], part(T.r1q, T.r1sc), part((T.r2q, T.r3q)[k], (T.r2sc, T.r3sc)[k]))
+            g.wait_ge(S.fp, len(far))
+            send([(s, far[:len(far) // 2], S.f), (peer, far[len(far) // 2:], S.f)],
+                 part(T.fq, T.fsc, lo, hi), part(T.fq, T.fsc, lo, hi))
+            send([(own, near, S.f)], part(T.fq, T.fsc, lo, hi), part(T.fq, T.fsc, lo, hi))
+            g.wait_ge(S.sent, sent[0])
+            return
+
+    for w in range(2):
+        if core in passer[h][w]:
+            j = passer[h][w].index(core)
+            s = single[h]
+            far, near = far_near(pair[h][0], s)
+
+            def part2(q, sc):
+                return sc[:] if j == 0 else codes(q)
+            if w == 0:
+                g.wait_ge(S.r2, len(far))
+                send([(pair[h][0], far[:len(far) // 2], S.e), (pair[h][1], far[len(far) // 2:], S.e)],
+                     part2(T.r2q, T.r2sc), part2(T.eq, T.esc))
+                send([(s, near, S.r1)], part2(T.r2q, T.r2sc), part2(T.r1q, T.r1sc))
+            else:
+                g.wait_ge(S.r1, len(near))
+                send([(pair[h][0], far[:len(far) // 2], S.e2), (pair[h][1], far[len(far) // 2:], S.e2)],
+                     part2(T.r1q, T.r1sc), part2(T.e2q, T.e2sc))
+            g.wait_ge(S.sent, sent[0])
+            return
 
     if T.rank_of(core) is None:
         return
 
     def piece(t, i):
         return t[:, W * i:W * i + W]
+
+    is_pair = core in pair[h]
+    k = pair[h].index(core) if is_pair else 0
+    order = [2 * (1 - k), 2 * (1 - k) + 1, 2 * k, 2 * k + 1] if is_pair else [0, 1, 2, 3]
     g.sync.dma_start(T.b_sb[:], T.b[:]).then_inc(S.ld_b, 16)
-    g.scalar.dma_start(piece(T.a_sb, 0), piece(T.a, 0)).then_inc(S.ld_a0, 16)
-    g.sync.dma_start(piece(T.a_sb, 1), piece(T.a, 1)).then_inc(S.ld_a1, 16)
-    g.scalar.dma_start(piece(T.a_sb, 2), piece(T.a, 2)).then_inc(S.ld_a2, 16)
-    g.sync.dma_start(piece(T.a_sb, 3), piece(T.a, 3)).then_inc(S.ld_a3, 16)
-    selectors()
+    for n, i in enumerate(order):
+        (g.scalar, g.sync)[n % 2].dma_start(piece(T.a_sb, i), piece(T.a, i)).then_inc(S["ld_a%d" % i], 16)
+    diagonal()
+    if is_pair:
+        g.vector.memset(T.te_bf[:], 0.0).then_inc(S.z1, 1)
     g.vector.wait_ge(S.ld_b, 16)
     g.vector.quantize_mx(T.bq[:], T.bsc[:], T.b_sb[:]).then_inc(S.bq, 1)
     g.tensor.wait_ge(S.bq, 1)
-    for i in range(4):
+
+    def load_product(i):
         g.vector.wait_ge(S["ld_a%d" % i], 16)
         g.vector.quantize_mx(T.aq[:, NC * i:NC * i + NC], T.asc[:, NC * i:NC * i + NC],
                              piece(T.a_sb, i)).then_inc(S["aq%d" % i], 1)
         g.tensor.wait_ge(S["aq%d" % i], 1)
         product(i, i, True).then_inc(S["g1_%d" % i], 1)
-    for i in range(3):
-        g.scalar.wait_ge(S["g1_%d" % i], 1)
-        g.scalar.activation(T.t_bf[:, i:W:4], bank(i), ActivationFunctionType.Copy).then_inc(S.cp1a, 1)
-    g.vector.wait_ge(S.g1_3, 1)
-    g.vector.tensor_copy(T.t_bf[:, 3:W:4], bank(3)).then_inc(S.cp1v, 1)
-    g.vector.wait_ge(S.cp1v, 1)
-    g.vector.wait_ge(S.cp1a, 3)
-    g.vector.quantize_mx(T.tq[:], T.tsc[:], T.t_bf[:]).then_inc(S.tq, 1)
-    for i in range(4):
-        product(i, 4 + i, False)
-    g.tensor.wait_ge(S.selq, 4)
-    g.wait_ge(S.tq, 1)
 
-    if core in pair[h]:
-        k = pair[h].index(core)
+    if is_pair:
         peer = pair[h][1 - k]
-        far, near = far_near(peer, relay[h][k])
+        far, near = far_near(peer, relay[h][k][0])
         lo, hi = HALF * k, HALF * k + HALF
-        tile([(peer, far, S.r1)], T.tq, T.tsc, T.r1q, T.r1sc)
-        tile([(relay[h][k], near, S.r1)], T.tq, T.tsc, T.r1q, T.r1sc)
+        load_product(order[0])
+        load_product(order[1])
+        g.scalar.wait_ge(S.z1, 1)
+        for u in range(2):
+            g.scalar.wait_ge(S["g1_%d" % order[u]], 1)
+            g.scalar.activation(T.te_bf[:, u:W:4], bank(order[u]), COPY).then_inc(S.cpe, 1)
+        g.vector.wait_ge(S.z1, 1)
+        g.vector.wait_ge(S.cpe, 2)
+        g.vector.quantize_mx(T.teq[:], T.tesc[:], T.te_bf[:]).then_inc(S.teq, 1)
+        g.wait_ge(S.teq, 1)
+        tile([(peer, far, S.r1)], T.teq, T.tesc, T.r1q, T.r1sc)
+        load_product(order[2])
+        load_product(order[3])
+        for n, i in enumerate(order):
+            if n >= 2:
+                g.scalar.wait_ge(S["g1_%d" % i], 1)
+            g.scalar.activation(place(T.t_bf, i), bank(i), COPY).then_inc(S.cp1a, 1)
+        g.vector.wait_ge(S.sel, 1)
+        selector(0, S.selq)
+        selector(1, S.selq)
+        g.vector.memset(T.o_bf[:], 0.0).then_inc(S.z2, 1)
+        g.vector.wait_ge(S.cp1a, 4)
+        g.vector.quantize_mx(T.tq[:], T.tsc[:], T.t_bf[:]).then_inc(S.tq, 1)
+        g.wait_ge(S.tq, 1)
+        send([(relay[h][k][0], near, S.r1)], T.tsc[:], T.r1sc[:])
+        send([(relay[h][k][1], near, S.r1)], codes(T.tq), codes(T.r1q))
+        for u in range(2):
+            product(2 * k + u, 4 + u, False)
+        g.tensor.wait_ge(S.selq, 2)
         g.tensor.wait_ge(S.r1, 2 * len(far))
-        for i in range(4):
-            unpack(i, 4 + i, T.r1q, T.r1sc, False, True).then_inc(S["g2_%d" % i], 1)
-        gather(T.o_bf, 4, "g2_%d", S.cp2a, S.cp2v)
-        g.vector.wait_ge(S.cp2a, 2)
-        g.vector.wait_ge(S.cp2v, 2)
+        for u in range(2):
+            unpack(u, 4 + u, T.r1q, T.r1sc, False, True).then_inc(S["g2_%d" % u], 1)
+        g.scalar.wait_ge(S.z2, 1)
+        g.scalar.wait_ge(S.g2_0, 1)
+        g.scalar.activation(place(T.o_bf, 2 * k), bank(4), COPY).then_inc(S.cp2a, 1)
+        g.vector.wait_ge(S.z2, 1)
+        g.vector.wait_ge(S.g2_1, 1)
+        g.vector.tensor_copy(place(T.o_bf, 2 * k + 1), bank(5)).then_inc(S.cp2v, 1)
+        g.vector.wait_ge(S.cp2a, 1)
+        g.vector.wait_ge(S.cp2v, 1)
         g.vector.quantize_mx(T.oq[:], T.osc[:], T.o_bf[:]).then_inc(S.oq, 1)
+        selector(2, S.selq2)
+        selector(3, S.selq2)
         g.wait_ge(S.oq, 1)
-        send([(relay[o][k], far, S.fp)], T.osc[:, lo:hi], T.fsc[:, lo:hi])
-        send([(relay[o][k], far, S.fc)], codes(T.oq, lo, hi), codes(T.fq, lo, hi))
-        g.tensor.wait_ge(S.cp1a, 3)
-        g.tensor.wait_ge(S.cp1v, 1)
+        send([(relay[o][k][0], far, S.fp)], T.osc[:, lo:hi], T.fsc[:, lo:hi])
+        send([(relay[o][k][1], far, S.fp)], codes(T.oq, lo, hi), codes(T.fq, lo, hi))
+        tile([(peer, far, S.n)], T.oq, T.osc, T.nq, T.nsc)
+        g.tensor.wait_ge(S.cpe, 2)
+        g.tensor.wait_ge(S.cp1a, 4)
+        g.tensor.wait_ge(S.oq, 1)
+        g.tensor.wait_ge(S.selq2, 2)
         for i in range(4):
-            product(i, i, False)
-            unpack(i, i, T.r1q, T.r1sc, False, False)
-        g.tensor.wait_ge(S.e, len(far))
-        for i in range(4):
-            unpack(i, i, T.eq, T.esc, False, False)
+            unpack(i, i, T.oq, T.osc, True, False)
+        for sem, n, q, sc in ((S.e, len(far), T.eq, T.esc), (S.e2, len(far), T.e2q, T.e2sc),
+                              (S.n, 2 * len(far), T.nq, T.nsc)):
+            g.tensor.wait_ge(sem, n)
+            for i in range(4):
+                unpack(i, i, q, sc, False, False)
         g.tensor.wait_ge(S.f, 2 * len(near) + len(far))
         for i in range(4):
             unpack(i, i, T.fq, T.fsc, False, True).then_inc(S["g3_%d" % i], 1)
         base = 0
     else:
-        far, near = far_near(adder[o], adder[h])
-        tile([(adder[o], far, S.r2)], T.tq, T.tsc, T.r2q, T.r2sc)
-        tile([(adder[h], near, S.r1)], T.tq, T.tsc, T.r1q, T.r1sc)
+        far, near = far_near(passer[o][0][0], passer[h][1][0])
+        for i in order:
+            load_product(i)
+        for i in range(3):
+            g.scalar.wait_ge(S["g1_%d" % i], 1)
+            g.scalar.activation(place(T.t_bf, i), bank(i), COPY).then_inc(S.cp1a, 1)
+        g.vector.wait_ge(S.g1_3, 1)
+        g.vector.tensor_copy(place(T.t_bf, 3), bank(3)).then_inc(S.cp1v, 1)
+        g.vector.wait_ge(S.cp1v, 1)
+        g.vector.wait_ge(S.cp1a, 3)
+        g.vector.quantize_mx(T.tq[:], T.tsc[:], T.t_bf[:]).then_inc(S.tq, 1)
+        g.vector.wait_ge(S.sel, 1)
+        for i in range(4):
+            selector(i, S.selq)
+        g.wait_ge(S.tq, 1)
+        send([(passer[o][0][0], far, S.r2)], T.tsc[:], T.r2sc[:])
+        send([(passer[o][0][1], far, S.r2)], codes(T.tq), codes(T.r2q))
+        send([(passer[h][1][0], near, S.r1)], T.tsc[:], T.r1sc[:])
+        send([(passer[h][1][1], near, S.r1)], codes(T.tq), codes(T.r1q))
+        g.tensor.wait_ge(S.tq, 1)
+        g.tensor.wait_ge(S.selq, 4)
+        for i in range(4):
+            unpack(i, 4 + i, T.tq, T.tsc, True, False)
         for sem, n, q, sc in ((S.r1, 2 * len(near), T.r1q, T.r1sc), (S.r2, 2 * len(far), T.r2q, T.r2sc),
                               (S.r3, 2 * len(far), T.r3q, T.r3sc)):
             g.tensor.wait_ge(sem, n)
@@ -239,9 +287,18 @@ def rank_program(g, core, T, topo):
             unpack(i, 4 + i, T.fq, T.fsc, False, True).then_inc(S["g3_%d" % i], 1)
         base = 4
 
-    gather(T.y_sb, base, "g3_%d", S.cp3a, S.cp3v)
-    g.sync.wait_ge(S.cp3a, 2)
-    g.sync.wait_ge(S.cp3v, 2)
+    for i in (0, 2):
+        g.scalar.wait_ge(S["g3_%d" % i], 1)
+        for hh in range(2):
+            g.scalar.activation(T.y_sb[:, 4 * (i // 2) + 2 * hh + i % 2:W:8],
+                                bank(base + i, HALF * hh, HALF * hh + HALF), COPY).then_inc(S.cp3a, 1)
+    for i in (1, 3):
+        g.vector.wait_ge(S["g3_%d" % i], 1)
+        for hh in range(2):
+            g.vector.tensor_copy(T.y_sb[:, 4 * (i // 2) + 2 * hh + i % 2:W:8],
+                                 bank(base + i, HALF * hh, HALF * hh + HALF)).then_inc(S.cp3v, 1)
+    g.sync.wait_ge(S.cp3a, 4)
+    g.sync.wait_ge(S.cp3v, 4)
     g.sync.dma_start(T.y[:], T.y_sb[:]).then_inc(S.ydone, 16)
     g.sync.wait_ge(S.ydone, 16)
     g.wait_ge(S.sent, sent[0])

from concourse.bass import DstId, RemoteDMATransfer
from concourse.mybir import dt, AluOpType, ActivationFunctionType

WORLD = 256
NC = 128
HALF = NC // 2
W = 4 * NC
BANK = 512

_CODES, _PLANE = "float8_e4m3fn_x4", "uint8"
SCRATCH = {
    "a_sb": ("sbuf", [128, 4 * W], "bfloat16"), "b_sb": ("sbuf", [128, W], "bfloat16"),
    "aq": ("sbuf", [128, 4 * NC], _CODES), "asc": ("sbuf", [128, 4 * NC], _PLANE),
    "bq": ("sbuf", [128, NC], _CODES), "bsc": ("sbuf", [128, NC], _PLANE),
    "diag": ("sbuf", [128, W + 4], "bfloat16"),
    "selq": ("sbuf", [128, 4 * NC], _CODES), "selsc": ("sbuf", [128, 4 * NC], _PLANE),
    "te_bf": ("sbuf", [128, W], "bfloat16"), "teq": ("sbuf", [128, NC], _CODES), "tesc": ("sbuf", [128, NC], _PLANE),
    "t_bf": ("sbuf", [128, W], "bfloat16"), "tq": ("sbuf", [128, NC], _CODES), "tsc": ("sbuf", [128, NC], _PLANE),
    "o_bf": ("sbuf", [128, W], "bfloat16"), "oq": ("sbuf", [128, NC], _CODES), "osc": ("sbuf", [128, NC], _PLANE),
    "r1q": ("sbuf", [128, NC], _CODES), "r1sc": ("sbuf", [128, NC], _PLANE),
    "r2q": ("sbuf", [128, NC], _CODES), "r2sc": ("sbuf", [128, NC], _PLANE),
    "r3q": ("sbuf", [128, NC], _CODES), "r3sc": ("sbuf", [128, NC], _PLANE),
    "nq": ("sbuf", [128, NC], _CODES), "nsc": ("sbuf", [128, NC], _PLANE),
    "eq": ("sbuf", [128, NC], _CODES), "esc": ("sbuf", [128, NC], _PLANE),
    "e2q": ("sbuf", [128, NC], _CODES), "e2sc": ("sbuf", [128, NC], _PLANE),
    "fq": ("sbuf", [128, NC], _CODES), "fsc": ("sbuf", [128, NC], _PLANE),
    "y_sb": ("sbuf", [128, W], "float32"),
    "ps": ("psum", [128, 8 * BANK], "float32"),
}
SEMAPHORES = (["ones", "sel", "selq", "selq2", "z1", "z2", "ld_b", "bq", "teq", "tq", "oq", "cpe", "cp1a", "cp1v",
               "cp2a", "cp2v", "cp3a", "cp3v", "r1", "r2", "r3", "n", "e", "e2", "fp", "f", "ydone", "sent"]
              + ["ld_a%d" % i for i in range(4)] + ["aq%d" % i for i in range(4)]
              + ["g1_%d" % i for i in range(4)] + ["g2_%d" % i for i in range(4)] + ["g3_%d" % i for i in range(4)])


def _bits(mask):
    return [e for e in range(16) if (mask >> e) & 1]


def _mask(engines):
    m = 0
    for e in engines:
        m |= 1 << e
    return m


def _plan(T, topo):
    cores = list(T.cores)
    hosts = sorted({topo.host(c) for c in cores})
    pair, single, relay, passer = {}, {}, {}, {}
    for h in hosts:
        mine = [c for c in cores if topo.host(c) == h]
        pair[h] = [[x, y] for x in mine for y in mine if x < y and topo.may_write(x, y) and topo.may_write(y, x)][0]
        single[h] = [c for c in mine if c not in pair[h]][0]

        def beside(c):
            return [k for k in range(WORLD) if k != c and topo.host(k) == h and topo.chip(k) == topo.chip(c)]
        relay[h] = [[k for k in beside(x) if topo.die(k) == topo.die(x) and topo.may_write(k, single[h])][:2]
                    for x in pair[h]]
        s = single[h]
        ok = [k for k in beside(s) if all(topo.may_write(k, x) for x in pair[h])]
        passer[h] = ([k for k in ok if topo.die(k) != topo.die(s)][:2], [k for k in ok if topo.die(k) == topo.die(s)][:2])
    return hosts, pair, single, relay, passer


def rank_program(g, core, T, topo):
    hosts, pair, single, relay, passer = _plan(T, topo)
    h = topo.host(core)
    if h not in hosts:
        return
    o = [x for x in hosts if x != h][0]
    S = T.sem
    sent = [0]
    COPY = ActivationFunctionType.Copy

    def codes(buf, lo=0, hi=NC):
        return buf[:, lo:hi].bitcast(dt.uint8)

    def send(dests, src, dst):
        if len(dests) == 1:
            d, engines, sem = dests[0]
            rid, pid = topo.addr(d, core)
            g.remote_dma(out_ap=dst, in_ap=src, remote_sem=sem, local_sem=S.sent, pid=pid, routing_id=rid,
                         dma_engine_mask=_mask(engines))
            sent[0] += len(engines)
            return
        tr = []
        for d, engines, sem in dests:
            rid, pid = topo.addr(d, core)
            tr.append(RemoteDMATransfer(dst_ids=[DstId(rid=rid, pnc=pid)], dma_engine_mask=_mask(engines),
                                        remote_sem=sem, src=src, dst=dst))
            sent[0] += len(engines)
        g.remote_dma_fused(tr, local_sem=S.sent)

    def tile(dests, sq, ssc, dq, dsc, lo=0, hi=NC):
        send(dests, ssc[:, lo:hi], dsc[:, lo:hi])
        send(dests, codes(sq, lo, hi), codes(dq, lo, hi))

    def far_near(far, near):
        f = _bits(topo.mask(core, far))
        return f, [e for e in _bits(topo.mask(core, near)) if e not in f]

    def bank(k, lo=0, hi=NC):
        return T.ps[:, BANK * k + lo:BANK * k + hi]

    def diagonal():
        g.vector.memset(T.diag[:], 1.0).then_inc(S.ones, 1)
        g.wait_ge(S.ones, 1)
        g.affine_select(T.diag[:], T.diag[:], [[-1, W + 4]], AluOpType.is_equal, 0.0, 3, 4).then_inc(S.sel, 1)

    def selector(i, sem):
        g.vector.quantize_mx(T.selq[:, NC * i:NC * i + NC], T.selsc[:, NC * i:NC * i + NC],
                             T.diag[:, 3 - i:3 - i + W]).then_inc(sem, 1)

    def unpack(i, k, q, sc, start, stop):
        return g.tensor.matmul_mx(bank(k), T.selq[:, NC * i:NC * i + NC], T.selsc[:, NC * i:NC * i + NC],
                                  q[:], sc[:], start, stop)

    def product(i, k, stop):
        return g.tensor.matmul_mx(bank(k), T.aq[:, NC * i:NC * i + NC], T.asc[:, NC * i:NC * i + NC],
                                  T.bq[:], T.bsc[:], True, stop)

    def place(t, i):
        return t[:, (W // 2) * (i // 2) + i % 2:(W // 2) * (i // 2) + W // 2:2]

    for k in range(2):
        if core in relay[h][k]:
            j = relay[h][k].index(core)
            own, peer, s = pair[h][k], pair[h][1 - k], single[h]
            far, near = far_near(s, own)
            lo, hi = HALF * k, HALF * k + HALF

            def part(q, sc, a=0, b=NC):
                return sc[:, a:b] if j == 0 else codes(q, a, b)
            g.wait_ge(S.r1, len(near))
            send([(s, far, (S.r2, S.r3)[k])], part(T.r1q, T.r1sc), part((T.r2q, T.r3q)[k], (T.r2sc, T.r3sc)[k]))
            g.wait_ge(S.fp, len(far))
            send([(s, far[:len(far) // 2], S.f), (peer, far[len(far) // 2:], S.f)],
                 part(T.fq, T.fsc, lo, hi), part(T.fq, T.fsc, lo, hi))
            send([(own, near, S.f)], part(T.fq, T.fsc, lo, hi), part(T.fq, T.fsc, lo, hi))
            g.wait_ge(S.sent, sent[0])
            return

    for w in range(2):
        if core in passer[h][w]:
            j = passer[h][w].index(core)
            s = single[h]
            far, near = far_near(pair[h][0], s)

            def part2(q, sc):
                return sc[:] if j == 0 else codes(q)
            if w == 0:
                g.wait_ge(S.r2, len(far))
                send([(pair[h][0], far[:len(far) // 2], S.e), (pair[h][1], far[len(far) // 2:], S.e)],
                     part2(T.r2q, T.r2sc), part2(T.eq, T.esc))
                send([(s, near, S.r1)], part2(T.r2q, T.r2sc), part2(T.r1q, T.r1sc))
            else:
                g.wait_ge(S.r1, len(near))
                send([(pair[h][0], far[:len(far) // 2], S.e2), (pair[h][1], far[len(far) // 2:], S.e2)],
                     part2(T.r1q, T.r1sc), part2(T.e2q, T.e2sc))
            g.wait_ge(S.sent, sent[0])
            return

    if T.rank_of(core) is None:
        return

    def piece(t, i):
        return t[:, W * i:W * i + W]

    is_pair = core in pair[h]
    k = pair[h].index(core) if is_pair else 0
    order = [2 * (1 - k), 2 * (1 - k) + 1, 2 * k, 2 * k + 1] if is_pair else [0, 1, 2, 3]
    g.sync.dma_start(T.b_sb[:], T.b[:]).then_inc(S.ld_b, 16)
    for n, i in enumerate(order):
        (g.scalar, g.sync)[n % 2].dma_start(piece(T.a_sb, i), piece(T.a, i)).then_inc(S["ld_a%d" % i], 16)
    diagonal()
    if is_pair:
        g.vector.memset(T.te_bf[:], 0.0).then_inc(S.z1, 1)
    g.vector.wait_ge(S.ld_b, 16)
    g.vector.quantize_mx(T.bq[:], T.bsc[:], T.b_sb[:]).then_inc(S.bq, 1)
    g.tensor.wait_ge(S.bq, 1)

    def load_product(i):
        g.vector.wait_ge(S["ld_a%d" % i], 16)
        g.vector.quantize_mx(T.aq[:, NC * i:NC * i + NC], T.asc[:, NC * i:NC * i + NC],
                             piece(T.a_sb, i)).then_inc(S["aq%d" % i], 1)
        g.tensor.wait_ge(S["aq%d" % i], 1)
        product(i, i, True).then_inc(S["g1_%d" % i], 1)

    if is_pair:
        peer = pair[h][1 - k]
        far, near = far_near(peer, relay[h][k][0])
        lo, hi = HALF * k, HALF * k + HALF
        load_product(order[0])
        load_product(order[1])
        g.scalar.wait_ge(S.z1, 1)
        for u in range(2):
            g.scalar.wait_ge(S["g1_%d" % order[u]], 1)
            g.scalar.activation(T.te_bf[:, u:W:4], bank(order[u]), COPY).then_inc(S.cpe, 1)
        g.vector.wait_ge(S.z1, 1)
        g.vector.wait_ge(S.cpe, 2)
        g.vector.quantize_mx(T.teq[:], T.tesc[:], T.te_bf[:]).then_inc(S.teq, 1)
        g.wait_ge(S.teq, 1)
        tile([(peer, far, S.r1)], T.teq, T.tesc, T.r1q, T.r1sc)
        load_product(order[2])
        load_product(order[3])
        for n, i in enumerate(order):
            if n >= 2:
                g.scalar.wait_ge(S["g1_%d" % i], 1)
            g.scalar.activation(place(T.t_bf, i), bank(i), COPY).then_inc(S.cp1a, 1)
        g.vector.wait_ge(S.sel, 1)
        selector(0, S.selq)
        selector(1, S.selq)
        g.vector.memset(T.o_bf[:], 0.0).then_inc(S.z2, 1)
        g.vector.wait_ge(S.cp1a, 4)
        g.vector.quantize_mx(T.tq[:], T.tsc[:], T.t_bf[:]).then_inc(S.tq, 1)
        g.wait_ge(S.tq, 1)
        send([(relay[h][k][0], near, S.r1)], T.tsc[:], T.r1sc[:])
        send([(relay[h][k][1], near, S.r1)], codes(T.tq), codes(T.r1q))
        for u in range(2):
            product(2 * k + u, 4 + u, False)
        g.tensor.wait_ge(S.selq, 2)
        g.tensor.wait_ge(S.r1, 2 * len(far))
        for u in range(2):
            unpack(u, 4 + u, T.r1q, T.r1sc, False, True).then_inc(S["g2_%d" % u], 1)
        g.scalar.wait_ge(S.z2, 1)
        g.scalar.wait_ge(S.g2_0, 1)
        g.scalar.activation(place(T.o_bf, 2 * k), bank(4), COPY).then_inc(S.cp2a, 1)
        g.vector.wait_ge(S.z2, 1)
        g.vector.wait_ge(S.g2_1, 1)
        g.vector.tensor_copy(place(T.o_bf, 2 * k + 1), bank(5)).then_inc(S.cp2v, 1)
        g.vector.wait_ge(S.cp2a, 1)
        g.vector.wait_ge(S.cp2v, 1)
        g.vector.quantize_mx(T.oq[:], T.osc[:], T.o_bf[:]).then_inc(S.oq, 1)
        selector(2, S.selq2)
        selector(3, S.selq2)
        g.wait_ge(S.oq, 1)
        send([(relay[o][k][0], far, S.fp)], T.osc[:, lo:hi], T.fsc[:, lo:hi])
        send([(relay[o][k][1], far, S.fp)], codes(T.oq, lo, hi), codes(T.fq, lo, hi))
        tile([(peer, far, S.n)], T.oq, T.osc, T.nq, T.nsc)
        g.tensor.wait_ge(S.cpe, 2)
        g.tensor.wait_ge(S.cp1a, 4)
        g.tensor.wait_ge(S.oq, 1)
        g.tensor.wait_ge(S.selq2, 2)
        for i in range(4):
            unpack(i, i, T.oq, T.osc, True, False)
        for sem, n, q, sc in ((S.e, len(far), T.eq, T.esc), (S.e2, len(far), T.e2q, T.e2sc),
                              (S.n, 2 * len(far), T.nq, T.nsc)):
            g.tensor.wait_ge(sem, n)
            for i in range(4):
                unpack(i, i, q, sc, False, False)
        g.tensor.wait_ge(S.f, 2 * len(near) + len(far))
        for i in range(4):
            unpack(i, i, T.fq, T.fsc, False, True).then_inc(S["g3_%d" % i], 1)
        base = 0
    else:
        far, near = far_near(passer[o][0][0], passer[h][1][0])
        for i in order:
            load_product(i)
        for i in range(3):
            g.scalar.wait_ge(S["g1_%d" % i], 1)
            g.scalar.activation(place(T.t_bf, i), bank(i), COPY).then_inc(S.cp1a, 1)
        g.vector.wait_ge(S.g1_3, 1)
        g.vector.tensor_copy(place(T.t_bf, 3), bank(3)).then_inc(S.cp1v, 1)
        g.vector.wait_ge(S.cp1v, 1)
        g.vector.wait_ge(S.cp1a, 3)
        g.vector.quantize_mx(T.tq[:], T.tsc[:], T.t_bf[:]).then_inc(S.tq, 1)
        g.vector.wait_ge(S.sel, 1)
        for i in range(4):
            selector(i, S.selq)
        g.wait_ge(S.tq, 1)
        send([(passer[o][0][0], far, S.r2)], T.tsc[:], T.r2sc[:])
        send([(passer[o][0][1], far, S.r2)], codes(T.tq), codes(T.r2q))
        send([(passer[h][1][0], near, S.r1)], T.tsc[:], T.r1sc[:])
        send([(passer[h][1][1], near, S.r1)], codes(T.tq), codes(T.r1q))
        g.tensor.wait_ge(S.tq, 1)
        g.tensor.wait_ge(S.selq, 4)
        for i in range(4):
            unpack(i, 4 + i, T.tq, T.tsc, True, False)
        for sem, n, q, sc in ((S.r1, 2 * len(near), T.r1q, T.r1sc), (S.r2, 2 * len(far), T.r2q, T.r2sc),
                              (S.r3, 2 * len(far), T.r3q, T.r3sc)):
            g.tensor.wait_ge(sem, n)
            for i in range(4):
                unpack(i, 4 + i, q, sc, False, False)
        g.tensor.wait_ge(S.f, 2 * len(far))
        for i in range(4):
            unpack(i, 4 + i, T.fq, T.fsc, False, True).then_inc(S["g3_%d" % i], 1)
        base = 4

    for i in (0, 2):
        g.scalar.wait_ge(S["g3_%d" % i], 1)
        for hh in range(2):
            g.scalar.activation(T.y_sb[:, 4 * (i // 2) + 2 * hh + i % 2:W:8],
                                bank(base + i, HALF * hh, HALF * hh + HALF), COPY).then_inc(S.cp3a, 1)
    for i in (1, 3):
        g.vector.wait_ge(S["g3_%d" % i], 1)
        for hh in range(2):
            g.vector.tensor_copy(T.y_sb[:, 4 * (i // 2) + 2 * hh + i % 2:W:8],
                                 bank(base + i, HALF * hh, HALF * hh + HALF)).then_inc(S.cp3v, 1)
    g.sync.wait_ge(S.cp3a, 4)
    g.sync.wait_ge(S.cp3v, 4)
    g.sync.dma_start(T.y[:], T.y_sb[:]).then_inc(S.ydone, 16)
    g.sync.wait_ge(S.ydone, 16)
    g.wait_ge(S.sent, sent[0])
